import numpy as np
import ml_dtypes


def mxq(x, axis, fmt="e4m3"):
    dtype, down = {"e4m3": (ml_dtypes.float8_e4m3fn, 7), "e5m2": (ml_dtypes.float8_e5m2, 14)}[fmt]
    v = np.moveaxis(np.asarray(x, np.float32).astype(ml_dtypes.bfloat16).astype(np.float64), axis, -1)
    blocks = v.reshape(v.shape[:-1] + (-1, 32))
    amax = np.abs(blocks).max(-1, keepdims=True)
    byte = np.maximum(np.where(amax > 0, np.frexp(amax)[1] - 1 + 127, 0) - down, 1)
    scale = np.exp2(byte - 127.0)
    codes = (blocks / scale).astype(np.float32).astype(dtype).astype(np.float64)
    return np.moveaxis((codes * scale).reshape(v.shape), -1, axis)


WIDE = False


def mx_kscale(k):
    if not WIDE:
        return np.ones(k)
    levels = np.array([10, -10, 5, -5, 0])
    if k % 512:
        return np.exp2(np.random.permutation(np.resize(levels, k // 32))).repeat(32)
    a = np.empty((k // 512, 16))
    for p in range(k // 512):
        a[p, :8] = np.random.permutation(np.resize(levels, 8))
        for g in range(8):
            far = levels[np.abs(levels - a[p, g]) >= 10]
            a[p, g + 8] = far[np.random.randint(len(far))]
    return np.exp2(a.ravel()).repeat(32)


def f64(x):
    return np.asarray(x).astype(np.float64)


def striped(idx):
    return np.tile(idx.reshape(-1, 16).T, (8, 1)).astype(np.uint16)


def unstriped(offs):
    return offs[:16].T.reshape(-1).astype(np.int64)


def pack_weight(w):
    k, n = w.shape
    w = f64(np.asarray(w, np.float32).astype(ml_dtypes.bfloat16)).reshape(k // 32, 32, n)
    amax = np.abs(w).max(1)
    byte = np.clip(np.where(amax > 0, np.frexp(amax)[1] - 1 + 127 - 7, 1), 1, 254)
    scaled = (w * np.exp2(127.0 - byte)[:, None, :]).reshape(k, n).astype(np.float32)
    words = np.ascontiguousarray(scaled.reshape(k // 512, 128, 4, n).transpose(0, 1, 3, 2)).astype(ml_dtypes.float8_e4m3fn).view(np.uint8)
    return words, np.ascontiguousarray(byte.astype(np.uint8).reshape(k // 512, 16, n))


def unpack_weight(words, scales):
    g, p, n, _ = words.shape
    vals = np.ascontiguousarray(words).view(ml_dtypes.float8_e4m3fn).astype(np.float64) * np.repeat(np.exp2(scales.astype(np.float64) - 127.0), 8, axis=1)[..., None]
    return vals.transpose(0, 1, 3, 2).reshape(g * 512, n)


E2M1 = np.array([0.0, 0.5, 1.0, 1.5, 2.0, 3.0, 4.0, 6.0, -0.0, -0.5, -1.0, -1.5, -2.0, -3.0, -4.0, -6.0])


def pack_fp4(w):
    k, n = w.shape
    w = f64(np.asarray(w, np.float32).astype(ml_dtypes.bfloat16)).reshape(k // 32, 32, n)
    amax = np.abs(w).max(1)
    mant, ex = np.frexp(amax / 6.0)
    byte = np.clip(np.where(amax > 0, np.where(mant > 0.5, ex, ex - 1) + 127, 1), 1, 254)
    scaled = (w * np.exp2(127.0 - byte)[:, None, :]).reshape(k, n).astype(np.float32)
    c = np.ascontiguousarray(scaled.reshape(k // 512, 128, 4, n).transpose(0, 1, 3, 2)).astype(ml_dtypes.float4_e2m1fn).view(np.uint8) & 0xF
    words = (c[..., 0::2] | (c[..., 1::2] << 4)).reshape(k // 512, 128, 2 * n)
    return np.ascontiguousarray(words), np.ascontiguousarray(byte.astype(np.uint8).reshape(k // 512, 16, n))


def unpack_fp4(words, scales):
    g, _, n = scales.shape
    words = np.ascontiguousarray(words).reshape(g, 128, n, 2)
    nib = np.empty((g, 128, n, 4), np.uint8)
    nib[..., 0::2] = words & 0xF
    nib[..., 1::2] = words >> 4
    vals = E2M1[nib] * np.repeat(np.exp2(scales.astype(np.float64) - 127.0), 8, axis=1)[..., None]
    return vals.transpose(0, 1, 3, 2).reshape(g * 512, n)


def planes(y):
    n, m = y.shape
    v = y.astype(np.float32).astype(ml_dtypes.bfloat16).astype(np.float64).reshape(n // 32, 32, m)
    top = np.abs(v).max(1)
    byte = np.clip(np.where(top > 0, np.frexp(top)[1] - 1 + 127 - 7, 1), 1, 254)
    codes = (v * np.exp2(127.0 - byte)[:, None, :]).reshape(n, m).astype(np.float32).astype(ml_dtypes.float8_e4m3fn).view(np.uint8)
    words = codes.reshape(n // 512, 128, 4, m).transpose(0, 1, 3, 2)
    return np.ascontiguousarray(words), np.ascontiguousarray(byte.astype(np.uint8).reshape(n // 512, 16, m))


K, T, S, N, H, U = 1024, 1024, 512, 512, 512, 1024


def setup_inputs():
    n = np.random.standard_normal
    s = mx_kscale(K)[:, None]
    u = mx_kscale(H)
    packed_xT = pack_weight(n((K, T)) * s)
    packed_w1 = pack_fp4(n((K, N)) / np.sqrt(K) / s)
    packed_w2 = pack_fp4(n((K, N)) / np.sqrt(K) / s)
    packed_w3 = pack_fp4(n((H, N)) / np.sqrt(H) / u[:, None])
    return {
        "x_words": packed_xT[0],
        "x_scales": packed_xT[1],
        "w1_words": packed_w1[0],
        "w1_scales": packed_w1[1],
        "w2_words": packed_w2[0],
        "w2_scales": packed_w2[1],
        "unit": (np.random.uniform(0.6, 1.4, (H, 1)) * u[:, None]).astype(np.float32),
        "w3_words": packed_w3[0],
        "w3_scales": packed_w3[1],
        "offs": striped(np.random.permutation(T)[:S]),
        "va": striped(np.random.permutation(np.concatenate([np.arange(S), np.random.randint(0, S, U - S)]))),
        "vb": striped(np.random.permutation(np.concatenate([np.arange(S), np.random.randint(0, S, U - S)]))),
        "vc": striped(np.random.permutation(np.concatenate([np.arange(S), np.random.randint(0, S, U - S)]))),
    }


def reference(x_words, x_scales, w1_words, w1_scales, w2_words, w2_scales, unit, w3_words, w3_scales, offs, va, vb, vc):
    xq = unpack_weight(x_words, x_scales)[:, unstriped(offs)]
    y = unpack_fp4(w1_words, w1_scales).T @ xq
    yva = y[:, unstriped(va)]
    yvb = y[:, unstriped(vb)]
    yvc = y[:, unstriped(vc)]
    cons = np.minimum(np.minimum(yva, yvb), yvc)
    z1 = unpack_fp4(w2_words, w2_scales).T @ xq
    zva = z1[:, unstriped(va)]
    zvb = z1[:, unstriped(vb)]
    zvc = z1[:, unstriped(vc)]
    hid = f64(unit) * (cons - (0.7 * (np.maximum(np.maximum(zva, zvb), zvc))))
    out_0 = unpack_fp4(w3_words, w3_scales).T @ mxq(hid, 0, "e4m3")
    return (out_0,) + planes(out_0)

@@ -1,0 +1,329 @@
+from contextlib import ExitStack
+
+import concourse.mybir as mybir
+from concourse.masks import make_identity
+
+K, T, S, H, N, U = 1024, 1024, 512, 512, 512, 1024
+FLOPS = 2 * K * H * S * 2 + 2 * H * N * U
+
+F32 = mybir.dt.float32
+BF16 = mybir.dt.bfloat16
+I32 = mybir.dt.int32
+U32 = mybir.dt.uint32
+U16 = mybir.dt.uint16
+U8 = mybir.dt.uint8
+FP8X4 = mybir.dt.float8_e4m3fn_x4
+FP4X4 = mybir.dt.float4_e2m1fn_x4
+COPY = mybir.ActivationFunctionType.Copy
+MIN = mybir.AluOpType.min
+MULT = mybir.AluOpType.mult
+
+P = 128
+PACK = 4
+PASSES = K // (P * PACK)
+ROW_TILES = H // P
+CHUNKS = (512, 384, 128)
+SPARE = 16
+SECOND_WEIGHT = 0.7
+SCALAR_TAKES_FIVE = 1
+
+
+def tile_picked_yvotepr_con_po_kernel(
+    tc, x_words, x_scales, w1_words, w1_scales, w2_words, w2_scales, unit, w3_words, w3_scales,
+    offs, va, vb, vc, out_0, out_1, out_2,
+):
+    nc = tc.nc
+    with ExitStack() as ctx:
+        keep = ctx.enter_context(tc.tile_pool(name="keep", bufs=1))
+        work = ctx.enter_context(tc.tile_pool(name="work", bufs=2))
+        psum = ctx.enter_context(tc.psum_pool(name="psum", bufs=1))
+
+        def load_list(src, name):
+            dst = keep.tile(list(src.shape), U16, name=name)
+            nc.sync.dma_start(dst[:], src)
+            return dst
+
+        def scale_tile(src, name, engine):
+            passes, rows, width = src.shape
+            dst = keep.tile([P, passes * width], U8, name=name, align_bytes=64)
+            engine.memset(dst[:].bitcast(I32), 0)
+            return dst
+
+        def load_scales(dst, src, queue):
+            passes = src.shape[0]
+            for q in range(4):
+                queue.dma_start(
+                    dst[32 * q : 32 * q + 4, :].bitcast(I32).rearrange("p (o c) -> p o c", o=passes),
+                    src[:, 4 * q : 4 * q + 4, :].bitcast(I32).rearrange("o q c -> q o c"),
+                )
+
+        def load_weight_words(src, name):
+            passes, rows, width = src.shape
+            dst = keep.tile([P, passes * width], U8, name=name, align_bytes=64)
+            nc.sync.dma_start(
+                dst[:].bitcast(I32).rearrange("p (o c) -> p o c", o=passes),
+                src.bitcast(I32).rearrange("o p c -> p o c"),
+            )
+            return dst
+
+        def load_x_words(o):
+            dst = keep.tile([P, T], U32, name="x_table%d" % o, align_bytes=64)
+            nc.sync.dma_start(dst[:].bitcast(I32), x_words[o].rearrange("p n t -> p (n t)").bitcast(I32))
+            return dst
+
+        xs_table = scale_tile(x_scales, "xs_table", nc.vector)
+        w1s = scale_tile(w1_scales, "w1s", nc.vector)
+        w2s = scale_tile(w2_scales, "w2s", nc.gpsimd)
+        w3s_raw = scale_tile(w3_scales, "w3s_raw", nc.vector)
+
+        offs_sb = load_list(offs, "offs_sb")
+        x_table = [load_x_words(0)]
+        load_scales(xs_table, x_scales, nc.sync)
+        x_table.append(load_x_words(1))
+        load_scales(w2s, w2_scales, nc.gpsimd)
+        w1w = load_weight_words(w1_words, "w1w")
+        load_scales(w1s, w1_scales, nc.sync)
+        w2w = load_weight_words(w2_words, "w2w")
+        va_sb = load_list(va, "va_sb")
+        vc_sb = load_list(vc, "vc_sb")
+        vb_sb = load_list(vb, "vb_sb")
+        unit4 = keep.tile([P, PACK], F32, name="unit4")
+        nc.sync.dma_start(unit4[:], unit.rearrange("(p t) o -> p (t o)", t=PACK))
+        w3w_raw = load_weight_words(w3_words, "w3w_raw")
+        load_scales(w3s_raw, w3_scales, nc.sync)
+
+        ident = keep.tile([P, P], F32, name="ident")
+        make_identity(nc, ident[:])
+
+        xq, xqs = [], []
+        for o in range(PASSES):
+            words = keep.tile([P, S], U32, name="xq%d" % o, align_bytes=64)
+            nc.vector.tensor_copy(words[:], x_table[o][:].indirect(offs_sb[:]))
+            picked_scales = keep.tile([P, S], U8, name="xqs%d" % o, align_bytes=64)
+            nc.vector.tensor_copy(picked_scales[:], xs_table[:, o * T : (o + 1) * T].indirect(offs_sb[:]))
+            xq.append(words)
+            xqs.append(picked_scales)
+
+        def project(words, scales, tau, factor, name, on_vector):
+            acc = psum.tile([P, S], F32, name="acc", tag="out", bufs=4)
+            for o in range(PASSES):
+                c0 = o * H + tau * P
+                nc.tensor.matmul_mx(
+                    acc[:],
+                    lhsT=words[:, 2 * c0 : 2 * (c0 + P)].bitcast(FP4X4),
+                    lhsT_scale=scales[:, c0 : c0 + P],
+                    rhs=xq[o][:].bitcast(FP8X4),
+                    rhs_scale=xqs[o][:],
+                    start=(o == 0),
+                    stop=(o == PASSES - 1),
+                )
+            window = keep.tile([P, S + SPARE], F32, name=name)
+            nc.gpsimd.memset(window[:, S:], 0.0)
+            if on_vector:
+                nc.vector.tensor_scalar_mul(window[:, :S], acc[:], factor)
+            else:
+                nc.scalar.activation(window[:, :S], acc[:], COPY, scale=factor)
+            return window
+
+        y_win, z_win = [], []
+
+        def project_tile(tau):
+            y_win.append(project(w1w, w1s, tau, 1.0, "y%d" % tau, False))
+            z_win.append(project(w2w, w2s, tau, -SECOND_WEIGHT, "z%d" % tau, tau == 0))
+
+        w3w = keep.tile([P, 2 * N], U8, name="w3w", align_bytes=64)
+        w3s = keep.tile([P, N], U8, name="w3s", align_bytes=64)
+
+        def deal_w3():
+            nc.vector.tensor_copy(
+                w3w[:].rearrange("p (t m b) -> p t m b", t=PACK, b=2),
+                w3w_raw[:].rearrange("p (m t b) -> p t m b", t=PACK, b=2),
+            )
+            nc.vector.tensor_copy(
+                w3s[:].rearrange("p (t m) -> p t m", t=PACK),
+                w3s_raw[:].rearrange("p (m t) -> p t m", t=PACK),
+            )
+
+        unit_row = keep.tile([P, H], F32, name="unit_row")
+
+        def spread_unit():
+            unit_ps = psum.tile([P, PACK, P], F32, name="unit_ps", tag="back", bufs=2)
+            for t in range(PACK):
+                nc.tensor.transpose(unit_ps[:, t, :], unit4[:, t : t + 1].to_broadcast([P, P]), ident[:])
+            nc.vector.tensor_copy(
+                unit_row[:].rearrange("r (p t) -> r p t", t=PACK), unit_ps[:].rearrange("r t p -> r p t")
+            )
+
+        out_scales = keep.tile([P, U], U8, name="out_scales", align_bytes=64)
+        starts = [sum(CHUNKS[:c]) for c in range(len(CHUNKS))]
+        units = [(c, tau) for c in range(len(CHUNKS)) for tau in range(ROW_TILES)]
+        state = {}
+
+        def entries(lst, c):
+            return lst[:, starts[c] // 16 : (starts[c] + CHUNKS[c]) // 16]
+
+        def gather(c, tau):
+            width = CHUNKS[c]
+            got = []
+            for name, lst in (("at_a", va_sb), ("at_b", vb_sb), ("at_c", vc_sb)):
+                g = work.tile([P, 2, width], F32, name=name)
+                for side, win in enumerate((y_win, z_win)):
+                    window = win[tau][:].indirect(entries(lst, c))
+                    if name == "at_c" and (side == 0 or tau != SCALAR_TAKES_FIVE):
+                        nc.vector.tensor_copy(g[:, side, :], window)
+                    else:
+                        nc.scalar.activation(g[:, side, :], window, COPY)
+                got.append(g)
+            state[("g", c, tau)] = got
+
+        def smaller_of_two(c, tau):
+            at_a, at_b, at_c = state[("g", c, tau)]
+            two = work.tile([P, 2, CHUNKS[c]], F32, name="two")
+            nc.vector.tensor_tensor(two[:], at_a[:], at_b[:], MIN)
+            state[("2", c, tau)] = two
+
+        def smallest(c, tau):
+            width = CHUNKS[c]
+            three = work.tile([P, 2, width], F32, name="three")
+            nc.vector.tensor_tensor(three[:], state[("2", c, tau)][:], state[("g", c, tau)][2][:], MIN)
+            ymin, zmin = three[:, 0, :], three[:, 1, :]
+            blocks = width // P
+            turned = psum.tile([P, blocks, P], F32, name="turned", tag="acc", bufs=2)
+            for b in range(blocks):
+                cols = slice(b * P, (b + 1) * P)
+                nc.tensor.matmul(turned[:, b, :], ymin[:, cols], ident[:], start=True, stop=False, is_transpose=True)
+                nc.tensor.matmul(turned[:, b, :], zmin[:, cols], ident[:], start=False, stop=True, is_transpose=True)
+            state[("t", c, tau)] = turned
+
+        def scale_and_round(c, tau):
+            blocks = CHUNKS[c] // P
+            if tau == 0:
+                state[("h", c)] = work.tile([P, blocks, H], BF16, name="hid_rows")
+            rows = slice(tau * P, (tau + 1) * P)
+            nc.vector.tensor_tensor(
+                state[("h", c)][:, :, rows],
+                state[("t", c, tau)][:],
+                unit_row[:, rows].unsqueeze(1).to_broadcast([P, blocks, P]),
+                MULT,
+            )
+
+        def turn_back(c):
+            width = CHUNKS[c]
+            blocks = width // P
+            grouped = work.tile([P, PACK * width], BF16, name="hid_grouped", align_bytes=64)
+            for b0 in range(0, blocks, 2):
+                nb = min(2, blocks - b0)
+                back = psum.tile([P, nb, 2, P], F32, name="back", tag="back", bufs=2)
+                for b in range(nb):
+                    pairs = state[("h", c)][:, b0 + b, :].bitcast(F32)
+                    for u in range(2):
+                        nc.tensor.transpose(back[:, b, u, :], pairs[:, u : H // 2 : 2], ident[:])
+                nc.vector.tensor_copy(
+                    grouped[:].bitcast(F32)[:, 2 * P * b0 : 2 * P * (b0 + nb)].rearrange("p (b r u) -> p b r u", b=nb, u=2),
+                    back[:].rearrange("p b u r -> p b r u"),
+                )
+            state[("q", c)] = grouped
+
+        def quantise_hidden(c):
+            width = CHUNKS[c]
+            codes = work.tile([P, width], U32, name="hid_codes", align_bytes=64)
+            scales = work.tile([P, width], U8, name="hid_scales", align_bytes=64)
+            nc.vector.quantize_mx(codes[:].bitcast(FP8X4), scales[:], state[("q", c)][:])
+            state[("c", c)] = (codes, scales)
+
+        def last_product(c):
+            width = CHUNKS[c]
+            codes, scales = state[("c", c)]
+            result = work.tile([P, PACK, width], F32, name="result")
+            pieces = [(0, 256), (256, width)] if width == 384 else [(0, width)]
+            for t in range(PACK):
+                bank = psum.tile([P, width], F32, name="bank", tag="out", bufs=4)
+                for lo, hi in pieces:
+                    nc.tensor.matmul_mx(
+                        bank[:, lo:hi],
+                        lhsT=w3w[:, 2 * P * t : 2 * P * (t + 1)].bitcast(FP4X4),
+                        lhsT_scale=w3s[:, P * t : P * (t + 1)],
+                        rhs=codes[:, lo:hi].bitcast(FP8X4),
+                        rhs_scale=scales[:, lo:hi],
+                        start=True,
+                        stop=True,
+                    )
+                nc.scalar.activation(result[:, t, :], bank[:], COPY)
+            cols = slice(starts[c], starts[c] + width)
+            nc.sync.dma_start(out_0.rearrange("(p t) r -> p t r", t=PACK)[:, :, cols], result[:])
+            state[("r", c)] = result
+
+        def last_block(c):
+            width = CHUNKS[c]
+            codes, scales = state[("c", c)]
+            bank = psum.tile([P, PACK, width], F32, name="bank", tag="out", bufs=4)
+            for t in range(PACK):
+                nc.tensor.matmul_mx(
+                    bank[:, t, :],
+                    lhsT=w3w[:, 2 * P * t : 2 * P * (t + 1)].bitcast(FP4X4),
+                    lhsT_scale=w3s[:, P * t : P * (t + 1)],
+                    rhs=codes[:].bitcast(FP8X4),
+                    rhs_scale=scales[:],
+                    start=True,
+                    stop=True,
+                )
+            grouped = work.tile([P, width, PACK], BF16, name="out_grouped", align_bytes=64)
+            nc.vector.tensor_copy(grouped[:], bank[:].rearrange("p t r -> p r t"))
+            state[("o", c)] = grouped
+            result = work.tile([P, PACK, width], F32, name="result")
+            nc.scalar.activation(result[:], bank[:], COPY)
+            cols = slice(starts[c], starts[c] + width)
+            nc.scalar.dma_start(out_0.rearrange("(p t) r -> p t r", t=PACK)[:, :, cols], result[:])
+
+        def regroup(c):
+            width = CHUNKS[c]
+            grouped = work.tile([P, width, PACK], BF16, name="out_grouped", align_bytes=64)
+            nc.vector.tensor_copy(grouped[:], state[("r", c)][:].rearrange("p t r -> p r t"))
+            state[("o", c)] = grouped
+
+        def hand_on(c):
+            width = CHUNKS[c]
+            cols = slice(starts[c], starts[c] + width)
+            grouped = state[("o", c)]
+            codes = work.tile([P, width], U32, name="out_codes", align_bytes=64)
+            nc.vector.quantize_mx(codes[:].bitcast(FP8X4), out_scales[:, cols], grouped[:].rearrange("p r t -> p (r t)"))
+            nc.sync.dma_start(
+                out_1[0].rearrange("p n t -> p (n t)").bitcast(I32)[:, cols], codes[:].bitcast(I32)
+            )
+
+        project_tile(0)
+        gather(*units[0])
+        for n, (c, tau) in enumerate(units):
+            if n + 1 < ROW_TILES:
+                project_tile(n + 1)
+            if n + 1 < len(units):
+                gather(*units[n + 1])
+            smaller_of_two(c, tau)
+            if n == 0:
+                spread_unit()
+            if n == 1:
+                deal_w3()
+            if n >= 1:
+                scale_and_round(*units[n - 1])
+            if c >= 2 and tau == 0:
+                regroup(c - 2)
+            if c >= 1 and tau == 1:
+                turn_back(c - 1)
+            smallest(c, tau)
+            if c >= 2 and tau == 0:
+                hand_on(c - 2)
+            if c >= 1 and tau == 1:
+                quantise_hidden(c - 1)
+                last_product(c - 1)
+        last = len(CHUNKS) - 1
+        regroup(last - 1)
+        scale_and_round(*units[-1])
+        hand_on(last - 1)
+        turn_back(last)
+        quantise_hidden(last)
+        last_block(last)
+        hand_on(last)
+        for q in range(4):
+            nc.sync.dma_start(
+                out_2[0, 4 * q : 4 * q + 4, :].bitcast(I32), out_scales[32 * q : 32 * q + 4, :].bitcast(I32)
+            )

@@ -25,7 +25,10 @@ ROW_TILES = H // P
 CHUNKS = (512, 384, 128)
 SPARE = 16
 SECOND_WEIGHT = 0.7
-SCALAR_TAKES_FIVE = 1
+VECTOR_SHARE = ((3, 2, 2, 2), (2, 1, 2, 1), (1, 1, 1, 1))
+AB_BUFS = 2
+BACK_ON_SCALAR = (0, 0, 0)
+C_BUFS = 2
 
 
 def tile_picked_yvotepr_con_po_kernel(
@@ -57,6 +60,13 @@ def tile_picked_yvotepr_con_po_kernel(
                     src[:, 4 * q : 4 * q + 4, :].bitcast(I32).rearrange("o q c -> q o c"),
                 )
 
+        def load_scale_table(o):
+            dst = keep.tile([P, T], U8, name="xs_table%d" % o, align_bytes=64)
+            for q in range(4):
+                rows = x_scales[o, 4 * q : 4 * q + 4, :].bitcast(I32)
+                nc.sync.dma_start(dst[32 * q : 32 * q + 32, :].bitcast(I32), rows.unsqueeze(0).to_broadcast([8, 4, T // 4]))
+            return dst
+
         def load_weight_words(src, name):
             passes, rows, width = src.shape
             dst = keep.tile([P, passes * width], U8, name=name, align_bytes=64)
@@ -71,19 +81,18 @@ def tile_picked_yvotepr_con_po_kernel(
             nc.sync.dma_start(dst[:].bitcast(I32), x_words[o].rearrange("p n t -> p (n t)").bitcast(I32))
             return dst
 
-        xs_table = scale_tile(x_scales, "xs_table", nc.vector)
-        w1s = scale_tile(w1_scales, "w1s", nc.vector)
-        w2s = scale_tile(w2_scales, "w2s", nc.gpsimd)
+        w1s = scale_tile(w1_scales, "w1s", nc.gpsimd)
+        w2s = scale_tile(w2_scales, "w2s", nc.vector)
         w3s_raw = scale_tile(w3_scales, "w3s_raw", nc.vector)
 
         offs_sb = load_list(offs, "offs_sb")
-        x_table = [load_x_words(0)]
-        load_scales(xs_table, x_scales, nc.sync)
-        x_table.append(load_x_words(1))
-        load_scales(w2s, w2_scales, nc.gpsimd)
+        xs_table = [load_scale_table(0)]
+        x_table = [load_x_words(0), load_x_words(1)]
         w1w = load_weight_words(w1_words, "w1w")
+        xs_table.append(load_scale_table(1))
         load_scales(w1s, w1_scales, nc.sync)
         w2w = load_weight_words(w2_words, "w2w")
+        load_scales(w2s, w2_scales, nc.sync)
         va_sb = load_list(va, "va_sb")
         vc_sb = load_list(vc, "vc_sb")
         vb_sb = load_list(vb, "vb_sb")
@@ -97,12 +106,13 @@ def tile_picked_yvotepr_con_po_kernel(
 
         xq, xqs = [], []
         for o in range(PASSES):
+            picked_scales = keep.tile([P, S], U8, name="xqs%d" % o, align_bytes=64)
+            nc.vector.tensor_copy(picked_scales[:], xs_table[o][:].indirect(offs_sb[:]))
+            xqs.append(picked_scales)
+        for o in range(PASSES):
             words = keep.tile([P, S], U32, name="xq%d" % o, align_bytes=64)
             nc.vector.tensor_copy(words[:], x_table[o][:].indirect(offs_sb[:]))
-            picked_scales = keep.tile([P, S], U8, name="xqs%d" % o, align_bytes=64)
-            nc.vector.tensor_copy(picked_scales[:], xs_table[:, o * T : (o + 1) * T].indirect(offs_sb[:]))
             xq.append(words)
-            xqs.append(picked_scales)
 
         def project(words, scales, tau, factor, name, on_vector):
             acc = psum.tile([P, S], F32, name="acc", tag="out", bufs=4)
@@ -129,17 +139,17 @@ def tile_picked_yvotepr_con_po_kernel(
 
         def project_tile(tau):
             y_win.append(project(w1w, w1s, tau, 1.0, "y%d" % tau, False))
-            z_win.append(project(w2w, w2s, tau, -SECOND_WEIGHT, "z%d" % tau, tau == 0))
+            z_win.append(project(w2w, w2s, tau, -SECOND_WEIGHT, "z%d" % tau, True))
 
         w3w = keep.tile([P, 2 * N], U8, name="w3w", align_bytes=64)
         w3s = keep.tile([P, N], U8, name="w3s", align_bytes=64)
 
         def deal_w3():
-            nc.vector.tensor_copy(
+            nc.gpsimd.tensor_copy(
                 w3w[:].rearrange("p (t m b) -> p t m b", t=PACK, b=2),
                 w3w_raw[:].rearrange("p (m t b) -> p t m b", t=PACK, b=2),
             )
-            nc.vector.tensor_copy(
+            nc.gpsimd.tensor_copy(
                 w3s[:].rearrange("p (t m) -> p t m", t=PACK),
                 w3s_raw[:].rearrange("p (m t) -> p t m", t=PACK),
             )
@@ -150,8 +160,8 @@ def tile_picked_yvotepr_con_po_kernel(
             unit_ps = psum.tile([P, PACK, P], F32, name="unit_ps", tag="back", bufs=2)
             for t in range(PACK):
                 nc.tensor.transpose(unit_ps[:, t, :], unit4[:, t : t + 1].to_broadcast([P, P]), ident[:])
-            nc.vector.tensor_copy(
-                unit_row[:].rearrange("r (p t) -> r p t", t=PACK), unit_ps[:].rearrange("r t p -> r p t")
+            nc.scalar.activation(
+                unit_row[:].rearrange("r (p t) -> r p t", t=PACK), unit_ps[:].rearrange("r t p -> r p t"), COPY
             )
 
         out_scales = keep.tile([P, U], U8, name="out_scales", align_bytes=64)
@@ -164,16 +174,16 @@ def tile_picked_yvotepr_con_po_kernel(
 
         def gather(c, tau):
             width = CHUNKS[c]
-            got = []
-            for name, lst in (("at_a", va_sb), ("at_b", vb_sb), ("at_c", vc_sb)):
-                g = work.tile([P, 2, width], F32, name=name)
-                for side, win in enumerate((y_win, z_win)):
+            got = [work.tile([P, 2, width], F32, name=name, bufs=bufs) for name, bufs in (("at_a", AB_BUFS), ("at_b", AB_BUFS), ("at_c", C_BUFS))]
+            share = VECTOR_SHARE[c][tau]
+            on_vector = [(True, 0), (True, 1)][:share]
+            for side, win in enumerate((y_win, z_win)):
+                for g, lst in zip(got, (va_sb, vb_sb, vc_sb)):
                     window = win[tau][:].indirect(entries(lst, c))
-                    if name == "at_c" and (side == 0 or tau != SCALAR_TAKES_FIVE):
+                    if (lst is vc_sb, side) in on_vector or (lst is vb_sb and side == 1 and share == 3):
                         nc.vector.tensor_copy(g[:, side, :], window)
                     else:
                         nc.scalar.activation(g[:, side, :], window, COPY)
-                got.append(g)
             state[("g", c, tau)] = got
 
         def smaller_of_two(c, tau):
@@ -218,7 +228,7 @@ def tile_picked_yvotepr_con_po_kernel(
                     pairs = state[("h", c)][:, b0 + b, :].bitcast(F32)
                     for u in range(2):
                         nc.tensor.transpose(back[:, b, u, :], pairs[:, u : H // 2 : 2], ident[:])
-                nc.vector.tensor_copy(
+                (nc.scalar.copy if BACK_ON_SCALAR[c] else nc.vector.tensor_copy)(
                     grouped[:].bitcast(F32)[:, 2 * P * b0 : 2 * P * (b0 + nb)].rearrange("p (b r u) -> p b r u", b=nb, u=2),
                     back[:].rearrange("p b u r -> p b r u"),
                 )
@@ -291,6 +301,7 @@ def tile_picked_yvotepr_con_po_kernel(
                 out_1[0].rearrange("p n t -> p (n t)").bitcast(I32)[:, cols], codes[:].bitcast(I32)
             )
 
+        last = len(CHUNKS) - 1
         project_tile(0)
         gather(*units[0])
         for n, (c, tau) in enumerate(units):
@@ -298,24 +309,23 @@ def tile_picked_yvotepr_con_po_kernel(
                 project_tile(n + 1)
             if n + 1 < len(units):
                 gather(*units[n + 1])
-            smaller_of_two(c, tau)
-            if n == 0:
-                spread_unit()
             if n == 1:
-                deal_w3()
+                spread_unit()
             if n >= 1:
                 scale_and_round(*units[n - 1])
-            if c >= 2 and tau == 0:
-                regroup(c - 2)
-            if c >= 1 and tau == 1:
+            smaller_of_two(c, tau)
+            if n == 1:
+                deal_w3()
+            if c >= 1 and tau == 0:
                 turn_back(c - 1)
+            if 1 <= c < last and tau == 3:
+                regroup(c - 1)
             smallest(c, tau)
-            if c >= 2 and tau == 0:
-                hand_on(c - 2)
-            if c >= 1 and tau == 1:
+            if c >= 1 and tau == 0:
                 quantise_hidden(c - 1)
                 last_product(c - 1)
-        last = len(CHUNKS) - 1
+            if 1 <= c < last and tau == 3:
+                hand_on(c - 1)
         regroup(last - 1)
         scale_and_round(*units[-1])
         hand_on(last - 1)

@@ -25,7 +25,7 @@ ROW_TILES = H // P
 CHUNKS = (512, 384, 128)
 SPARE = 16
 SECOND_WEIGHT = 0.7
-VECTOR_SHARE = ((3, 2, 2, 2), (2, 1, 2, 1), (1, 1, 1, 1))
+VECTOR_SHARE = ((3, 2, 2, 2), (2, 2, 1, 1), (1, 1, 1, 1))
 AB_BUFS = 2
 BACK_ON_SCALAR = (0, 0, 0)
 C_BUFS = 2
@@ -88,58 +88,59 @@ def tile_picked_yvotepr_con_po_kernel(
         offs_sb = load_list(offs, "offs_sb")
         xs_table = [load_scale_table(0)]
         x_table = [load_x_words(0), load_x_words(1)]
-        w1w = load_weight_words(w1_words, "w1w")
-        xs_table.append(load_scale_table(1))
-        load_scales(w1s, w1_scales, nc.sync)
-        w2w = load_weight_words(w2_words, "w2w")
-        load_scales(w2s, w2_scales, nc.sync)
-        va_sb = load_list(va, "va_sb")
-        vc_sb = load_list(vc, "vc_sb")
-        vb_sb = load_list(vb, "vb_sb")
         unit4 = keep.tile([P, PACK], F32, name="unit4")
         nc.sync.dma_start(unit4[:], unit.rearrange("(p t) o -> p (t o)", t=PACK))
+        xs_table.append(load_scale_table(1))
+        w1w = load_weight_words(w1_words, "w1w")
+        load_scales(w1s, w1_scales, nc.sync)
+        va_sb = load_list(va, "va_sb")
+        w2w = load_weight_words(w2_words, "w2w")
+        load_scales(w2s, w2_scales, nc.sync)
+        vc_sb = load_list(vc, "vc_sb")
+        vb_sb = load_list(vb, "vb_sb")
         w3w_raw = load_weight_words(w3_words, "w3w_raw")
         load_scales(w3s_raw, w3_scales, nc.sync)
 
         ident = keep.tile([P, P], F32, name="ident")
         make_identity(nc, ident[:])
 
-        xq, xqs = [], []
+        xq = [keep.tile([P, S], U32, name="xq%d" % o, align_bytes=64) for o in range(PASSES)]
+        xqs = [keep.tile([P, S], U8, name="xqs%d" % o, align_bytes=64) for o in range(PASSES)]
+        halves = [slice(0, S // 2), slice(S // 2, S)]
+        nc.vector.tensor_copy(xqs[0][:], xs_table[0][:].indirect(offs_sb[:]))
         for o in range(PASSES):
-            picked_scales = keep.tile([P, S], U8, name="xqs%d" % o, align_bytes=64)
-            nc.vector.tensor_copy(picked_scales[:], xs_table[o][:].indirect(offs_sb[:]))
-            xqs.append(picked_scales)
-        for o in range(PASSES):
-            words = keep.tile([P, S], U32, name="xq%d" % o, align_bytes=64)
-            nc.vector.tensor_copy(words[:], x_table[o][:].indirect(offs_sb[:]))
-            xq.append(words)
+            nc.vector.tensor_copy(xq[o][:], x_table[o][:].indirect(offs_sb[:]))
+        for half in halves:
+            nc.vector.tensor_copy(xqs[1][:, half], xs_table[1][:].indirect(offs_sb[:, half.start // 16 : half.stop // 16]))
 
-        def project(words, scales, tau, factor, name, on_vector):
-            acc = psum.tile([P, S], F32, name="acc", tag="out", bufs=4)
+        def new_window(name):
+            window = keep.tile([P, S + SPARE], F32, name=name)
+            nc.gpsimd.memset(window[:, S:], 0.0)
+            return window
+
+        y_win = [new_window("y%d" % tau) for tau in range(ROW_TILES)]
+        z_win = [new_window("z%d" % tau) for tau in range(ROW_TILES)]
+
+        def project(words, scales, tau, cols):
+            acc = psum.tile([P, cols.stop - cols.start], F32, name="acc", tag="acc" if tau == 0 else "out", bufs=2 if tau == 0 else 4)
             for o in range(PASSES):
                 c0 = o * H + tau * P
                 nc.tensor.matmul_mx(
                     acc[:],
                     lhsT=words[:, 2 * c0 : 2 * (c0 + P)].bitcast(FP4X4),
                     lhsT_scale=scales[:, c0 : c0 + P],
-                    rhs=xq[o][:].bitcast(FP8X4),
-                    rhs_scale=xqs[o][:],
+                    rhs=xq[o][:, cols].bitcast(FP8X4),
+                    rhs_scale=xqs[o][:, cols],
                     start=(o == 0),
                     stop=(o == PASSES - 1),
                 )
-            window = keep.tile([P, S + SPARE], F32, name=name)
-            nc.gpsimd.memset(window[:, S:], 0.0)
-            if on_vector:
-                nc.vector.tensor_scalar_mul(window[:, :S], acc[:], factor)
-            else:
-                nc.scalar.activation(window[:, :S], acc[:], COPY, scale=factor)
-            return window
-
-        y_win, z_win = [], []
+            return acc
 
         def project_tile(tau):
-            y_win.append(project(w1w, w1s, tau, 1.0, "y%d" % tau, False))
-            z_win.append(project(w2w, w2s, tau, -SECOND_WEIGHT, "z%d" % tau, True))
+            for cols in halves if tau == 0 else [slice(0, S)]:
+                nc.scalar.activation(y_win[tau][:, cols], project(w1w, w1s, tau, cols)[:], COPY)
+            for cols in halves if tau == 0 else [slice(0, S)]:
+                nc.vector.tensor_scalar_mul(z_win[tau][:, cols], project(w2w, w2s, tau, cols)[:], -SECOND_WEIGHT)
 
         w3w = keep.tile([P, 2 * N], U8, name="w3w", align_bytes=64)
         w3s = keep.tile([P, N], U8, name="w3s", align_bytes=64)
@@ -277,18 +278,19 @@ def tile_picked_yvotepr_con_po_kernel(
                     start=True,
                     stop=True,
                 )
-            grouped = work.tile([P, width, PACK], BF16, name="out_grouped", align_bytes=64)
-            nc.vector.tensor_copy(grouped[:], bank[:].rearrange("p t r -> p r t"))
-            state[("o", c)] = grouped
             result = work.tile([P, PACK, width], F32, name="result")
             nc.scalar.activation(result[:], bank[:], COPY)
             cols = slice(starts[c], starts[c] + width)
             nc.scalar.dma_start(out_0.rearrange("(p t) r -> p t r", t=PACK)[:, :, cols], result[:])
+            state[("r", c)] = result
 
         def regroup(c):
             width = CHUNKS[c]
             grouped = work.tile([P, width, PACK], BF16, name="out_grouped", align_bytes=64)
-            nc.vector.tensor_copy(grouped[:], state[("r", c)][:].rearrange("p t r -> p r t"))
+            if c == len(CHUNKS) - 2:
+                nc.scalar.activation(grouped[:], state[("r", c)][:].rearrange("p t r -> p r t"), COPY)
+            else:
+                nc.vector.tensor_copy(grouped[:], state[("r", c)][:].rearrange("p t r -> p r t"))
             state[("o", c)] = grouped
 
         def hand_on(c):
@@ -332,8 +334,9 @@ def tile_picked_yvotepr_con_po_kernel(
         turn_back(last)
         quantise_hidden(last)
         last_block(last)
+        regroup(last)
         hand_on(last)
         for q in range(4):
-            nc.sync.dma_start(
+            (nc.sync if q < 2 else nc.scalar).dma_start(
                 out_2[0, 4 * q : 4 * q + 4, :].bitcast(I32), out_scales[32 * q : 32 * q + 4, :].bitcast(I32)
             )

@@ -25,10 +25,17 @@ ROW_TILES = H // P
 CHUNKS = (512, 384, 128)
 SPARE = 16
 SECOND_WEIGHT = 0.7
-VECTOR_SHARE = ((3, 2, 2, 2), (2, 2, 1, 1), (1, 1, 1, 1))
-AB_BUFS = 2
+VECTOR_SHARE = ((3, 2, 2, 2), (2, 2, 2, 1), (1, 1, 1, 1))
+AB_BUFS = 3
+TWO_BUFS = 2
+THREE_BUFS = 3
+RESULT_TAG = ("result", "at_b")
+FINISH_AT = 8
+EMPTY_AT = (5, 10)
+ACC_BUFS = 2
+Z_ON_VECTOR = 4
 BACK_ON_SCALAR = (0, 0, 0)
-C_BUFS = 2
+C_BUFS = 3
 
 
 def tile_picked_yvotepr_con_po_kernel(
@@ -122,7 +129,7 @@ def tile_picked_yvotepr_con_po_kernel(
         z_win = [new_window("z%d" % tau) for tau in range(ROW_TILES)]
 
         def project(words, scales, tau, cols):
-            acc = psum.tile([P, cols.stop - cols.start], F32, name="acc", tag="acc" if tau == 0 else "out", bufs=2 if tau == 0 else 4)
+            acc = psum.tile([P, cols.stop - cols.start], F32, name="acc", tag="low", bufs=2)
             for o in range(PASSES):
                 c0 = o * H + tau * P
                 nc.tensor.matmul_mx(
@@ -139,8 +146,11 @@ def tile_picked_yvotepr_con_po_kernel(
         def project_tile(tau):
             for cols in halves if tau == 0 else [slice(0, S)]:
                 nc.scalar.activation(y_win[tau][:, cols], project(w1w, w1s, tau, cols)[:], COPY)
-            for cols in halves if tau == 0 else [slice(0, S)]:
-                nc.vector.tensor_scalar_mul(z_win[tau][:, cols], project(w2w, w2s, tau, cols)[:], -SECOND_WEIGHT)
+            for cols in [slice(0, S)]:
+                if tau < Z_ON_VECTOR:
+                    nc.vector.tensor_scalar_mul(z_win[tau][:, cols], project(w2w, w2s, tau, cols)[:], -SECOND_WEIGHT)
+                else:
+                    nc.scalar.activation(z_win[tau][:, cols], project(w2w, w2s, tau, cols)[:], COPY, scale=-SECOND_WEIGHT)
 
         w3w = keep.tile([P, 2 * N], U8, name="w3w", align_bytes=64)
         w3s = keep.tile([P, N], U8, name="w3s", align_bytes=64)
@@ -189,17 +199,17 @@ def tile_picked_yvotepr_con_po_kernel(
 
         def smaller_of_two(c, tau):
             at_a, at_b, at_c = state[("g", c, tau)]
-            two = work.tile([P, 2, CHUNKS[c]], F32, name="two")
+            two = work.tile([P, 2, CHUNKS[c]], F32, name="two", bufs=TWO_BUFS)
             nc.vector.tensor_tensor(two[:], at_a[:], at_b[:], MIN)
             state[("2", c, tau)] = two
 
         def smallest(c, tau):
             width = CHUNKS[c]
-            three = work.tile([P, 2, width], F32, name="three")
+            three = work.tile([P, 2, width], F32, name="three", bufs=THREE_BUFS)
             nc.vector.tensor_tensor(three[:], state[("2", c, tau)][:], state[("g", c, tau)][2][:], MIN)
             ymin, zmin = three[:, 0, :], three[:, 1, :]
             blocks = width // P
-            turned = psum.tile([P, blocks, P], F32, name="turned", tag="acc", bufs=2)
+            turned = psum.tile([P, blocks, P], F32, name="turned", tag="acc", bufs=ACC_BUFS)
             for b in range(blocks):
                 cols = slice(b * P, (b + 1) * P)
                 nc.tensor.matmul(turned[:, b, :], ymin[:, cols], ident[:], start=True, stop=False, is_transpose=True)
@@ -245,10 +255,10 @@ def tile_picked_yvotepr_con_po_kernel(
         def last_product(c):
             width = CHUNKS[c]
             codes, scales = state[("c", c)]
-            result = work.tile([P, PACK, width], F32, name="result")
+            banks = []
             pieces = [(0, 256), (256, width)] if width == 384 else [(0, width)]
             for t in range(PACK):
-                bank = psum.tile([P, width], F32, name="bank", tag="out", bufs=4)
+                bank = psum.tile([P, width], F32, name="bank", tag="low" if t < 2 else "high", bufs=2)
                 for lo, hi in pieces:
                     nc.tensor.matmul_mx(
                         bank[:, lo:hi],
@@ -259,6 +269,14 @@ def tile_picked_yvotepr_con_po_kernel(
                         start=True,
                         stop=True,
                     )
+                banks.append(bank)
+            state[("b", c)] = banks
+
+        def empty_banks(c):
+            width = CHUNKS[c]
+            tag = RESULT_TAG[c]
+            result = work.tile([P, PACK, width], F32, name="result", tag=tag, bufs={"at_b": AB_BUFS, "at_a": AB_BUFS, "at_c": C_BUFS, "result": 2}[tag])
+            for t, bank in enumerate(state[("b", c)]):
                 nc.scalar.activation(result[:, t, :], bank[:], COPY)
             cols = slice(starts[c], starts[c] + width)
             nc.sync.dma_start(out_0.rearrange("(p t) r -> p t r", t=PACK)[:, :, cols], result[:])
@@ -267,7 +285,7 @@ def tile_picked_yvotepr_con_po_kernel(
         def last_block(c):
             width = CHUNKS[c]
             codes, scales = state[("c", c)]
-            bank = psum.tile([P, PACK, width], F32, name="bank", tag="out", bufs=4)
+            bank = psum.tile([P, PACK, width], F32, name="bank", tag="high", bufs=2)
             for t in range(PACK):
                 nc.tensor.matmul_mx(
                     bank[:, t, :],
@@ -311,6 +329,8 @@ def tile_picked_yvotepr_con_po_kernel(
                 project_tile(n + 1)
             if n + 1 < len(units):
                 gather(*units[n + 1])
+            if n in EMPTY_AT:
+                empty_banks(EMPTY_AT.index(n))
             if n == 1:
                 spread_unit()
             if n >= 1:
@@ -320,14 +340,14 @@ def tile_picked_yvotepr_con_po_kernel(
                 deal_w3()
             if c >= 1 and tau == 0:
                 turn_back(c - 1)
-            if 1 <= c < last and tau == 3:
-                regroup(c - 1)
+            if n == FINISH_AT:
+                regroup(0)
             smallest(c, tau)
             if c >= 1 and tau == 0:
                 quantise_hidden(c - 1)
                 last_product(c - 1)
-            if 1 <= c < last and tau == 3:
-                hand_on(c - 1)
+            if n == FINISH_AT:
+                hand_on(0)
         regroup(last - 1)
         scale_and_round(*units[-1])
         hand_on(last - 1)

from contextlib import ExitStack

import concourse.mybir as mybir
from concourse.masks import make_identity

K, T, S, H, N, U = 1024, 1024, 512, 512, 512, 1024
FLOPS = 2 * K * H * S * 2 + 2 * H * N * U

F32 = mybir.dt.float32
BF16 = mybir.dt.bfloat16
I32 = mybir.dt.int32
U32 = mybir.dt.uint32
U16 = mybir.dt.uint16
U8 = mybir.dt.uint8
FP8X4 = mybir.dt.float8_e4m3fn_x4
FP4X4 = mybir.dt.float4_e2m1fn_x4
COPY = mybir.ActivationFunctionType.Copy
MIN = mybir.AluOpType.min
MULT = mybir.AluOpType.mult

P = 128
PACK = 4
PASSES = K // (P * PACK)
ROW_TILES = H // P
CHUNKS = (512, 384, 128)
SPARE = 16
SECOND_WEIGHT = 0.7
VECTOR_SHARE = ((3, 2, 2, 2), (2, 2, 2, 1), (1, 1, 1, 1))
AB_BUFS = 3
TWO_BUFS = 2
THREE_BUFS = 3
RESULT_TAG = ("result", "at_b")
FINISH_AT = 8
EMPTY_AT = (5, 10)
ACC_BUFS = 2
Z_ON_VECTOR = 4
BACK_ON_SCALAR = (0, 0, 0)
C_BUFS = 3


def tile_picked_yvotepr_con_po_kernel(
    tc, x_words, x_scales, w1_words, w1_scales, w2_words, w2_scales, unit, w3_words, w3_scales,
    offs, va, vb, vc, out_0, out_1, out_2,
):
    nc = tc.nc
    with ExitStack() as ctx:
        keep = ctx.enter_context(tc.tile_pool(name="keep", bufs=1))
        work = ctx.enter_context(tc.tile_pool(name="work", bufs=2))
        psum = ctx.enter_context(tc.psum_pool(name="psum", bufs=1))

        def load_list(src, name):
            dst = keep.tile(list(src.shape), U16, name=name)
            nc.sync.dma_start(dst[:], src)
            return dst

        def scale_tile(src, name, engine):
            passes, rows, width = src.shape
            dst = keep.tile([P, passes * width], U8, name=name, align_bytes=64)
            engine.memset(dst[:].bitcast(I32), 0)
            return dst

        def load_scales(dst, src, queue):
            passes = src.shape[0]
            for q in range(4):
                queue.dma_start(
                    dst[32 * q : 32 * q + 4, :].bitcast(I32).rearrange("p (o c) -> p o c", o=passes),
                    src[:, 4 * q : 4 * q + 4, :].bitcast(I32).rearrange("o q c -> q o c"),
                )

        def load_scale_table(o):
            dst = keep.tile([P, T], U8, name="xs_table%d" % o, align_bytes=64)
            for q in range(4):
                rows = x_scales[o, 4 * q : 4 * q + 4, :].bitcast(I32)
                nc.sync.dma_start(dst[32 * q : 32 * q + 32, :].bitcast(I32), rows.unsqueeze(0).to_broadcast([8, 4, T // 4]))
            return dst

        def load_weight_words(src, name):
            passes, rows, width = src.shape
            dst = keep.tile([P, passes * width], U8, name=name, align_bytes=64)
            nc.sync.dma_start(
                dst[:].bitcast(I32).rearrange("p (o c) -> p o c", o=passes),
                src.bitcast(I32).rearrange("o p c -> p o c"),
            )
            return dst

        def load_x_words(o):
            dst = keep.tile([P, T], U32, name="x_table%d" % o, align_bytes=64)
            nc.sync.dma_start(dst[:].bitcast(I32), x_words[o].rearrange("p n t -> p (n t)").bitcast(I32))
            return dst

        w1s = scale_tile(w1_scales, "w1s", nc.gpsimd)
        w2s = scale_tile(w2_scales, "w2s", nc.vector)
        w3s_raw = scale_tile(w3_scales, "w3s_raw", nc.vector)

        offs_sb = load_list(offs, "offs_sb")
        xs_table = [load_scale_table(0)]
        x_table = [load_x_words(0), load_x_words(1)]
        unit4 = keep.tile([P, PACK], F32, name="unit4")
        nc.sync.dma_start(unit4[:], unit.rearrange("(p t) o -> p (t o)", t=PACK))
        xs_table.append(load_scale_table(1))
        w1w = load_weight_words(w1_words, "w1w")
        load_scales(w1s, w1_scales, nc.sync)
        va_sb = load_list(va, "va_sb")
        w2w = load_weight_words(w2_words, "w2w")
        load_scales(w2s, w2_scales, nc.sync)
        vc_sb = load_list(vc, "vc_sb")
        vb_sb = load_list(vb, "vb_sb")
        w3w_raw = load_weight_words(w3_words, "w3w_raw")
        load_scales(w3s_raw, w3_scales, nc.sync)

        ident = keep.tile([P, P], F32, name="ident")
        make_identity(nc, ident[:])

        xq = [keep.tile([P, S], U32, name="xq%d" % o, align_bytes=64) for o in range(PASSES)]
        xqs = [keep.tile([P, S], U8, name="xqs%d" % o, align_bytes=64) for o in range(PASSES)]
        halves = [slice(0, S // 2), slice(S // 2, S)]
        nc.vector.tensor_copy(xqs[0][:], xs_table[0][:].indirect(offs_sb[:]))
        for o in range(PASSES):
            nc.vector.tensor_copy(xq[o][:], x_table[o][:].indirect(offs_sb[:]))
        for half in halves:
            nc.vector.tensor_copy(xqs[1][:, half], xs_table[1][:].indirect(offs_sb[:, half.start // 16 : half.stop // 16]))

        def new_window(name):
            window = keep.tile([P, S + SPARE], F32, name=name)
            nc.gpsimd.memset(window[:, S:], 0.0)
            return window

        y_win = [new_window("y%d" % tau) for tau in range(ROW_TILES)]
        z_win = [new_window("z%d" % tau) for tau in range(ROW_TILES)]

        def project(words, scales, tau, cols):
            acc = psum.tile([P, cols.stop - cols.start], F32, name="acc", tag="low", bufs=2)
            for o in range(PASSES):
                c0 = o * H + tau * P
                nc.tensor.matmul_mx(
                    acc[:],
                    lhsT=words[:, 2 * c0 : 2 * (c0 + P)].bitcast(FP4X4),
                    lhsT_scale=scales[:, c0 : c0 + P],
                    rhs=xq[o][:, cols].bitcast(FP8X4),
                    rhs_scale=xqs[o][:, cols],
                    start=(o == 0),
                    stop=(o == PASSES - 1),
                )
            return acc

        def project_tile(tau):
            for cols in halves if tau == 0 else [slice(0, S)]:
                nc.scalar.activation(y_win[tau][:, cols], project(w1w, w1s, tau, cols)[:], COPY)
            for cols in [slice(0, S)]:
                if tau < Z_ON_VECTOR:
                    nc.vector.tensor_scalar_mul(z_win[tau][:, cols], project(w2w, w2s, tau, cols)[:], -SECOND_WEIGHT)
                else:
                    nc.scalar.activation(z_win[tau][:, cols], project(w2w, w2s, tau, cols)[:], COPY, scale=-SECOND_WEIGHT)

        w3w = keep.tile([P, 2 * N], U8, name="w3w", align_bytes=64)
        w3s = keep.tile([P, N], U8, name="w3s", align_bytes=64)

        def deal_w3():
            nc.gpsimd.tensor_copy(
                w3w[:].rearrange("p (t m b) -> p t m b", t=PACK, b=2),
                w3w_raw[:].rearrange("p (m t b) -> p t m b", t=PACK, b=2),
            )
            nc.gpsimd.tensor_copy(
                w3s[:].rearrange("p (t m) -> p t m", t=PACK),
                w3s_raw[:].rearrange("p (m t) -> p t m", t=PACK),
            )

        unit_row = keep.tile([P, H], F32, name="unit_row")

        def spread_unit():
            unit_ps = psum.tile([P, PACK, P], F32, name="unit_ps", tag="back", bufs=2)
            for t in range(PACK):
                nc.tensor.transpose(unit_ps[:, t, :], unit4[:, t : t + 1].to_broadcast([P, P]), ident[:])
            nc.scalar.activation(
                unit_row[:].rearrange("r (p t) -> r p t", t=PACK), unit_ps[:].rearrange("r t p -> r p t"), COPY
            )

        out_scales = keep.tile([P, U], U8, name="out_scales", align_bytes=64)
        starts = [sum(CHUNKS[:c]) for c in range(len(CHUNKS))]
        units = [(c, tau) for c in range(len(CHUNKS)) for tau in range(ROW_TILES)]
        state = {}

        def entries(lst, c):
            return lst[:, starts[c] // 16 : (starts[c] + CHUNKS[c]) // 16]

        def gather(c, tau):
            width = CHUNKS[c]
            got = [work.tile([P, 2, width], F32, name=name, bufs=bufs) for name, bufs in (("at_a", AB_BUFS), ("at_b", AB_BUFS), ("at_c", C_BUFS))]
            share = VECTOR_SHARE[c][tau]
            on_vector = [(True, 0), (True, 1)][:share]
            for side, win in enumerate((y_win, z_win)):
                for g, lst in zip(got, (va_sb, vb_sb, vc_sb)):
                    window = win[tau][:].indirect(entries(lst, c))
                    if (lst is vc_sb, side) in on_vector or (lst is vb_sb and side == 1 and share == 3):
                        nc.vector.tensor_copy(g[:, side, :], window)
                    else:
                        nc.scalar.activation(g[:, side, :], window, COPY)
            state[("g", c, tau)] = got

        def smaller_of_two(c, tau):
            at_a, at_b, at_c = state[("g", c, tau)]
            two = work.tile([P, 2, CHUNKS[c]], F32, name="two", bufs=TWO_BUFS)
            nc.vector.tensor_tensor(two[:], at_a[:], at_b[:], MIN)
            state[("2", c, tau)] = two

        def smallest(c, tau):
            width = CHUNKS[c]
            three = work.tile([P, 2, width], F32, name="three", bufs=THREE_BUFS)
            nc.vector.tensor_tensor(three[:], state[("2", c, tau)][:], state[("g", c, tau)][2][:], MIN)
            ymin, zmin = three[:, 0, :], three[:, 1, :]
            blocks = width // P
            turned = psum.tile([P, blocks, P], F32, name="turned", tag="acc", bufs=ACC_BUFS)
            for b in range(blocks):
                cols = slice(b * P, (b + 1) * P)
                nc.tensor.matmul(turned[:, b, :], ymin[:, cols], ident[:], start=True, stop=False, is_transpose=True)
                nc.tensor.matmul(turned[:, b, :], zmin[:, cols], ident[:], start=False, stop=True, is_transpose=True)
            state[("t", c, tau)] = turned

        def scale_and_round(c, tau):
            blocks = CHUNKS[c] // P
            if tau == 0:
                state[("h", c)] = work.tile([P, blocks, H], BF16, name="hid_rows")
            rows = slice(tau * P, (tau + 1) * P)
            nc.vector.tensor_tensor(
                state[("h", c)][:, :, rows],
                state[("t", c, tau)][:],
                unit_row[:, rows].unsqueeze(1).to_broadcast([P, blocks, P]),
                MULT,
            )

        def turn_back(c):
            width = CHUNKS[c]
            blocks = width // P
            grouped = work.tile([P, PACK * width], BF16, name="hid_grouped", align_bytes=64)
            for b0 in range(0, blocks, 2):
                nb = min(2, blocks - b0)
                back = psum.tile([P, nb, 2, P], F32, name="back", tag="back", bufs=2)
                for b in range(nb):
                    pairs = state[("h", c)][:, b0 + b, :].bitcast(F32)
                    for u in range(2):
                        nc.tensor.transpose(back[:, b, u, :], pairs[:, u : H // 2 : 2], ident[:])
                (nc.scalar.copy if BACK_ON_SCALAR[c] else nc.vector.tensor_copy)(
                    grouped[:].bitcast(F32)[:, 2 * P * b0 : 2 * P * (b0 + nb)].rearrange("p (b r u) -> p b r u", b=nb, u=2),
                    back[:].rearrange("p b u r -> p b r u"),
                )
            state[("q", c)] = grouped

        def quantise_hidden(c):
            width = CHUNKS[c]
            codes = work.tile([P, width], U32, name="hid_codes", align_bytes=64)
            scales = work.tile([P, width], U8, name="hid_scales", align_bytes=64)
            nc.vector.quantize_mx(codes[:].bitcast(FP8X4), scales[:], state[("q", c)][:])
            state[("c", c)] = (codes, scales)

        def last_product(c):
            width = CHUNKS[c]
            codes, scales = state[("c", c)]
            banks = []
            pieces = [(0, 256), (256, width)] if width == 384 else [(0, width)]
            for t in range(PACK):
                bank = psum.tile([P, width], F32, name="bank", tag="low" if t < 2 else "high", bufs=2)
                for lo, hi in pieces:
                    nc.tensor.matmul_mx(
                        bank[:, lo:hi],
                        lhsT=w3w[:, 2 * P * t : 2 * P * (t + 1)].bitcast(FP4X4),
                        lhsT_scale=w3s[:, P * t : P * (t + 1)],
                        rhs=codes[:, lo:hi].bitcast(FP8X4),
                        rhs_scale=scales[:, lo:hi],
                        start=True,
                        stop=True,
                    )
                banks.append(bank)
            state[("b", c)] = banks

        def empty_banks(c):
            width = CHUNKS[c]
            tag = RESULT_TAG[c]
            result = work.tile([P, PACK, width], F32, name="result", tag=tag, bufs={"at_b": AB_BUFS, "at_a": AB_BUFS, "at_c": C_BUFS, "result": 2}[tag])
            for t, bank in enumerate(state[("b", c)]):
                nc.scalar.activation(result[:, t, :], bank[:], COPY)
            cols = slice(starts[c], starts[c] + width)
            nc.sync.dma_start(out_0.rearrange("(p t) r -> p t r", t=PACK)[:, :, cols], result[:])
            state[("r", c)] = result

        def last_block(c):
            width = CHUNKS[c]
            codes, scales = state[("c", c)]
            bank = psum.tile([P, PACK, width], F32, name="bank", tag="high", bufs=2)
            for t in range(PACK):
                nc.tensor.matmul_mx(
                    bank[:, t, :],
                    lhsT=w3w[:, 2 * P * t : 2 * P * (t + 1)].bitcast(FP4X4),
                    lhsT_scale=w3s[:, P * t : P * (t + 1)],
                    rhs=codes[:].bitcast(FP8X4),
                    rhs_scale=scales[:],
                    start=True,
                    stop=True,
                )
            result = work.tile([P, PACK, width], F32, name="result")
            nc.scalar.activation(result[:], bank[:], COPY)
            cols = slice(starts[c], starts[c] + width)
            nc.scalar.dma_start(out_0.rearrange("(p t) r -> p t r", t=PACK)[:, :, cols], result[:])
            state[("r", c)] = result

        def regroup(c):
            width = CHUNKS[c]
            grouped = work.tile([P, width, PACK], BF16, name="out_grouped", align_bytes=64)
            if c == len(CHUNKS) - 2:
                nc.scalar.activation(grouped[:], state[("r", c)][:].rearrange("p t r -> p r t"), COPY)
            else:
                nc.vector.tensor_copy(grouped[:], state[("r", c)][:].rearrange("p t r -> p r t"))
            state[("o", c)] = grouped

        def hand_on(c):
            width = CHUNKS[c]
            cols = slice(starts[c], starts[c] + width)
            grouped = state[("o", c)]
            codes = work.tile([P, width], U32, name="out_codes", align_bytes=64)
            nc.vector.quantize_mx(codes[:].bitcast(FP8X4), out_scales[:, cols], grouped[:].rearrange("p r t -> p (r t)"))
            nc.sync.dma_start(
                out_1[0].rearrange("p n t -> p (n t)").bitcast(I32)[:, cols], codes[:].bitcast(I32)
            )

        last = len(CHUNKS) - 1
        project_tile(0)
        gather(*units[0])
        for n, (c, tau) in enumerate(units):
            if n + 1 < ROW_TILES:
                project_tile(n + 1)
            if n + 1 < len(units):
                gather(*units[n + 1])
            if n in EMPTY_AT:
                empty_banks(EMPTY_AT.index(n))
            if n == 1:
                spread_unit()
            if n >= 1:
                scale_and_round(*units[n - 1])
            smaller_of_two(c, tau)
            if n == 1:
                deal_w3()
            if c >= 1 and tau == 0:
                turn_back(c - 1)
            if n == FINISH_AT:
                regroup(0)
            smallest(c, tau)
            if c >= 1 and tau == 0:
                quantise_hidden(c - 1)
                last_product(c - 1)
            if n == FINISH_AT:
                hand_on(0)
        regroup(last - 1)
        scale_and_round(*units[-1])
        hand_on(last - 1)
        turn_back(last)
        quantise_hidden(last)
        last_block(last)
        regroup(last)
        hand_on(last)
        for q in range(4):
            (nc.sync if q < 2 else nc.scalar).dma_start(
                out_2[0, 4 * q : 4 * q + 4, :].bitcast(I32), out_scales[32 * q : 32 * q + 4, :].bitcast(I32)
            )
